import numpy as np
import ml_dtypes


def mxq(x, axis, fmt="e4m3"):
    dtype, down = {"e4m3": (ml_dtypes.float8_e4m3fn, 7), "e5m2": (ml_dtypes.float8_e5m2, 14)}[fmt]
    v = np.moveaxis(np.asarray(x, np.float32).astype(ml_dtypes.bfloat16).astype(np.float64), axis, -1)
    blocks = v.reshape(v.shape[:-1] + (-1, 32))
    amax = np.abs(blocks).max(-1, keepdims=True)
    byte = np.maximum(np.where(amax > 0, np.frexp(amax)[1] - 1 + 127, 0) - down, 1)
    scale = np.exp2(byte - 127.0)
    codes = (blocks / scale).astype(np.float32).astype(dtype).astype(np.float64)
    return np.moveaxis((codes * scale).reshape(v.shape), -1, axis)


WIDE = False


def mx_kscale(k):
    if not WIDE:
        return np.ones(k)
    levels = np.array([10, -10, 5, -5, 0])
    if k % 512:
        return np.exp2(np.random.permutation(np.resize(levels, k // 32))).repeat(32)
    a = np.empty((k // 512, 16))
    for p in range(k // 512):
        a[p, :8] = np.random.permutation(np.resize(levels, 8))
        for g in range(8):
            far = levels[np.abs(levels - a[p, g]) >= 10]
            a[p, g + 8] = far[np.random.randint(len(far))]
    return np.exp2(a.ravel()).repeat(32)


def f64(x):
    return np.asarray(x).astype(np.float64)


def striped8(idx):
    return np.asarray(idx).reshape(8, -1, 16).transpose(0, 2, 1).reshape(128, -1).astype(np.uint16)


def unstriped8(offs):
    return offs.reshape(8, 16, -1).transpose(0, 2, 1).reshape(8, -1).astype(np.int64)


def pick8(x, idx, run):
    r = np.arange(len(x))
    return x[r[:, None], idx[r % (8 * run) // run]]


E2M1 = np.array([0.0, 0.5, 1.0, 1.5, 2.0, 3.0, 4.0, 6.0, -0.0, -0.5, -1.0, -1.5, -2.0, -3.0, -4.0, -6.0])


def pack_weight(w, fmt):
    k, n = w.shape
    w = f64(np.asarray(w, np.float32).astype(ml_dtypes.bfloat16)).reshape(k // 32, 32, n)
    amax = np.abs(w).max(1)
    if fmt == "e4m3":
        byte = np.frexp(amax)[1] - 1 + 127 - 7
    else:
        mant, ex = np.frexp(amax / 6.0)
        byte = np.where(mant > 0.5, ex, ex - 1) + 127
    byte = np.clip(np.where(amax > 0, byte, 1), 1, 254)
    scaled = (w * np.exp2(127.0 - byte)[:, None, :]).reshape(k, n).astype(np.float32)
    by_word = np.ascontiguousarray(scaled.reshape(k // 512, 128, 4, n).transpose(0, 1, 3, 2))
    if fmt == "e4m3":
        words = by_word.astype(ml_dtypes.float8_e4m3fn).view(np.uint8)
    else:
        c = by_word.astype(ml_dtypes.float4_e2m1fn).view(np.uint8) & 0xF
        words = (c[..., 0::2] | (c[..., 1::2] << 4)).reshape(k // 512, 128, 2 * n)
    return np.ascontiguousarray(words), np.ascontiguousarray(byte.astype(np.uint8).reshape(k // 512, 16, n))


def unpack_weight(words, scales, fmt):
    g, _, n = scales.shape
    words = np.ascontiguousarray(words).reshape(g, 128, n, -1)
    if fmt == "e4m3":
        vals = words.view(ml_dtypes.float8_e4m3fn).astype(np.float64)
    else:
        nib = np.empty((g, 128, n, 4), np.uint8)
        nib[..., 0::2] = words & 0xF
        nib[..., 1::2] = words >> 4
        vals = E2M1[nib]
    vals = vals * np.repeat(np.exp2(scales.astype(np.float64) - 127.0), 8, axis=1)[..., None]
    return vals.transpose(0, 1, 3, 2).reshape(g * 512, n)


D, K, T, U, X, S, I, Q = 512, 512, 1024, 1024, 1024, 1024, 512, 128


def setup_inputs():
    n = np.random.standard_normal
    idx = np.stack([np.random.permutation(T)[:I] for _ in range(8)])
    idx2 = np.stack([np.random.permutation(U)[:I] for _ in range(8)])
    idx3 = np.stack([np.random.permutation(X)[:I] for _ in range(8)])
    idx4 = np.stack([np.random.permutation(S)[:I] for _ in range(8)])
    idx5 = np.stack([np.random.permutation(U)[:I] for _ in range(8)])
    idx6 = np.stack([np.random.permutation(S)[:I] for _ in range(8)])
    fd = mx_kscale(D)
    fk = mx_kscale(K)
    wqp = pack_weight(n((D, K)) * 1.0 / np.sqrt(D) * fd[:, None] * fk, "e4m3")
    keysp = pack_weight(n((K, T)) * 1.0 / np.sqrt(K) / fk[:, None], "e2m1")
    notesp = pack_weight(n((K, U)) * 1.0 / np.sqrt(K) / fk[:, None], "e4m3")
    usersp = pack_weight(n((D, X)) * 1.0 / np.sqrt(D) * fd[:, None], "e2m1")
    shelvesp = pack_weight(n((D, S)) * 1.0 / np.sqrt(D) * fd[:, None], "e4m3")
    return {
        "states": (n((D, Q)) * 0.95 / fd[:, None]).astype(np.float32),
        "wq_words": wqp[0],
        "wq_scales": wqp[1],
        "keys_words": keysp[0],
        "keys_scales": keysp[1],
        "notes_words": notesp[0],
        "notes_scales": notesp[1],
        "users_words": usersp[0],
        "users_scales": usersp[1],
        "shelves_words": shelvesp[0],
        "shelves_scales": shelvesp[1],
        "offs": striped8(idx),
        "offs2": striped8(idx2),
        "offs3": striped8(idx3),
        "offs4": striped8(idx4),
        "offs5": striped8(idx5),
        "offs6": striped8(idx6),
    }


def reference(states, wq_words, wq_scales, keys_words, keys_scales, notes_words, notes_scales, users_words, users_scales, shelves_words, shelves_scales, offs, offs2, offs3, offs4, offs5, offs6):
    idx = unstriped8(offs)
    idx2 = unstriped8(offs2)
    idx3 = unstriped8(offs3)
    idx4 = unstriped8(offs4)
    idx5 = unstriped8(offs5)
    idx6 = unstriped8(offs6)
    wqu = unpack_weight(wq_words, wq_scales, "e4m3")
    keysu = unpack_weight(keys_words, keys_scales, "e2m1")
    notesu = unpack_weight(notes_words, notes_scales, "e4m3")
    usersu = unpack_weight(users_words, users_scales, "e2m1")
    shelvesu = unpack_weight(shelves_words, shelves_scales, "e4m3")
    statesq = mxq(f64(states), 0, "e4m3")
    qv = wqu.T @ statesq
    qvq = mxq(qv, 0, "e4m3")
    a = qvq.T @ keysu
    b = qvq.T @ notesu
    c0 = statesq.T @ usersu
    d0 = statesq.T @ shelvesu
    f1 = np.zeros((Q, U))
    f1[np.arange(Q)[:, None], idx2[np.arange(Q) % 128 // 16]] = pick8(a, idx, 16)
    f2 = np.zeros((Q, S))
    f2[np.arange(Q)[:, None], idx4[np.arange(Q) % 128 // 16]] = pick8(c0, idx3, 16)
    bb = b + f1
    dd = d0 - f2
    y = np.maximum(pick8(bb, idx5, 16), pick8(dd, idx6, 16))
    return y

@@ -1,0 +1,175 @@
+from contextlib import ExitStack
+
+import concourse.mybir as mybir
+from concourse.masks import make_identity
+
+F32 = mybir.dt.float32
+BF16 = mybir.dt.bfloat16
+I32 = mybir.dt.int32
+U32 = mybir.dt.uint32
+U16 = mybir.dt.uint16
+U8 = mybir.dt.uint8
+FP8X4 = mybir.dt.float8_e4m3fn_x4
+FP4X4 = mybir.dt.float4_e2m1fn_x4
+COPY = mybir.ActivationFunctionType.Copy
+ALU = mybir.AluOpType
+
+P = 128
+PACK = 4
+Q = 128
+KQ = 512
+POOL = 1024
+SLOTS = 512
+BANK = 512
+HALF = SLOTS // 2
+LCOLS = SLOTS // 16
+
+FLOPS = 2 * 512 * Q * (KQ + 4 * POOL)
+
+
+def tile_attend_twomarkets_madefour_kernel(
+    tc, states, wq_words, wq_scales, keys_words, keys_scales, notes_words, notes_scales,
+    users_words, users_scales, shelves_words, shelves_scales,
+    offs, offs2, offs3, offs4, offs5, offs6, out,
+):
+    nc = tc.nc
+    with ExitStack() as ctx:
+        sb = ctx.enter_context(tc.tile_pool(name="sb", bufs=1))
+        ps = ctx.enter_context(tc.psum_pool(name="ps", bufs=1))
+
+        def load_list(src, name):
+            t = sb.tile([P, LCOLS], U16, name=name)
+            nc.sync.dma_start(t[:], src)
+            return t
+
+        def load_words8(src, width, name):
+            t = sb.tile([P, width], U32, name=name, align_bytes=64)
+            nc.sync.dma_start(t[:].bitcast(I32), src[0].rearrange("p n t -> p (n t)").bitcast(I32))
+            return t
+
+        def load_words4(src, name):
+            t = sb.tile([P, 2 * POOL], U8, name=name, align_bytes=64)
+            nc.sync.dma_start(t[:].bitcast(I32), src[0].bitcast(I32))
+            return t
+
+        def load_plane(queue, src, width, name):
+            t = sb.tile([P, width], U8, name=name, align_bytes=64)
+            for g in range(4):
+                queue.dma_start(t[32 * g : 32 * g + 4, :].bitcast(I32), src[0, 4 * g : 4 * g + 4, :].bitcast(I32))
+            return t
+
+        def half(lst, h):
+            return lst[:, h * (LCOLS // 2) : (h + 1) * (LCOLS // 2)]
+
+        st_raw = sb.tile([P, PACK, Q], F32, name="st_raw")
+        nc.sync.dma_start(st_raw[:], states.rearrange("(p j) q -> p j q", j=PACK))
+        users_s = load_plane(nc.scalar, users_scales, POOL, "users_s")
+        users_w = load_words4(users_words, "users_w")
+        wq_w = load_words8(wq_words, KQ, "wq_w")
+        wq_s = load_plane(nc.sync, wq_scales, KQ, "wq_s")
+        l3 = load_list(offs3, "l3")
+        l4 = load_list(offs4, "l4")
+        keys_w = load_words4(keys_words, "keys_w")
+        keys_s = load_plane(nc.sync, keys_scales, POOL, "keys_s")
+        shelves_w = load_words8(shelves_words, POOL, "shelves_w")
+        shelves_s = load_plane(nc.sync, shelves_scales, POOL, "shelves_s")
+        l1 = load_list(offs, "l1")
+        l2 = load_list(offs2, "l2")
+        notes_w = load_words8(notes_words, POOL, "notes_w")
+        notes_s = load_plane(nc.sync, notes_scales, POOL, "notes_s")
+        l6 = load_list(offs6, "l6")
+        l5 = load_list(offs5, "l5")
+
+        ident = sb.tile([P, P], F32, name="ident")
+        make_identity(nc, ident[:])
+
+        f2 = sb.tile([P, POOL], F32, name="f2")
+        f1 = sb.tile([P, POOL], F32, name="f1")
+        nc.vector.memset(f2[:], 0.0)
+        nc.vector.memset(f1[:], 0.0)
+
+        st_b = sb.tile([P, Q, PACK], BF16, name="st_b", align_bytes=64)
+        nc.vector.tensor_copy(st_b[:], st_raw[:].rearrange("p j q -> p q j"))
+        st_w = sb.tile([P, Q], U32, name="st_w", align_bytes=64)
+        st_s = sb.tile([P, Q], U8, name="st_s", align_bytes=64)
+        nc.vector.quantize_mx(st_w[:].bitcast(FP8X4), st_s[:], st_b[:].rearrange("p q j -> p (q j)"))
+
+        def score(bank, lhs_w, lhs_s, rhs, rhs_s):
+            nc.tensor.matmul_mx(bank, lhsT=lhs_w, lhsT_scale=lhs_s, rhs=rhs, rhs_scale=rhs_s, start=True, stop=True)
+
+        def fp4(words, lo, hi):
+            return words[:, 2 * lo : 2 * hi].bitcast(FP4X4)
+
+        def fp8(words, lo, hi):
+            return words[:, lo:hi].bitcast(FP8X4)
+
+        c0 = sb.tile([P, POOL], F32, name="c0")
+        quarter = POOL // 4
+        for j in range(4):
+            lo, hi = j * quarter, (j + 1) * quarter
+            bank = ps.tile([P, quarter], F32, name="c0_ps", tag="bank%d" % j)
+            score(bank[:], st_w[:].bitcast(FP8X4), st_s[:], fp4(users_w, lo, hi), users_s[:, lo:hi])
+            if j % 2 == 0:
+                nc.scalar.activation(c0[:, lo:hi], bank[:], COPY)
+            else:
+                nc.vector.tensor_copy(c0[:, lo:hi], bank[:])
+
+        qt_ps = ps.tile([P, KQ], F32, name="qt_ps", tag="bank4")
+        score(qt_ps[:], st_w[:].bitcast(FP8X4), st_s[:], fp8(wq_w, 0, KQ), wq_s[:])
+
+        cg0 = sb.tile([P, HALF], F32, name="cg0")
+        nc.vector.tensor_copy(cg0[:], c0[:].indirect(half(l3, 0)))
+        nc.vector.tensor_copy(f2[:].indirect(half(l4, 0)), cg0[:])
+
+        qt_b = sb.tile([P, 2, P, 2], BF16, name="qt_b", tag="qt_b")
+        nc.scalar.activation(qt_b[:], qt_ps[:].rearrange("q (p u e) -> q u p e", u=2, e=2), COPY)
+        qt_words = qt_b[:].rearrange("q u p e -> q (u p e)").bitcast(F32)
+        qv_ps = ps.tile([P, 2, Q], F32, name="qv_ps", tag="bank5")
+        for u in range(2):
+            nc.tensor.transpose(qv_ps[:, u, :], qt_words[:, u * P : (u + 1) * P], ident[:])
+        qv_b = sb.tile([P, Q * PACK], BF16, name="qv_b", align_bytes=64)
+        nc.scalar.copy(qv_b[:].bitcast(F32).rearrange("p (q u) -> p q u", u=2), qv_ps[:].rearrange("p u q -> p q u"))
+        qv_w = sb.tile([P, Q], U32, name="qv_w", align_bytes=64)
+        qv_s = sb.tile([P, Q], U8, name="qv_s", align_bytes=64)
+        nc.vector.quantize_mx(qv_w[:].bitcast(FP8X4), qv_s[:], qv_b[:])
+
+        cg1 = sb.tile([P, HALF], F32, name="cg1", tag="qt_b")
+        nc.scalar.activation(cg1[:], c0[:].indirect(half(l3, 1)), COPY)
+        nc.vector.tensor_copy(f2[:].indirect(half(l4, 1)), cg1[:])
+        a = sb.tile([P, POOL], F32, name="a", tag="a")
+        for j in range(4):
+            lo, hi = j * quarter, (j + 1) * quarter
+            bank = ps.tile([P, quarter], F32, name="a_ps", tag="bank%d" % j)
+            score(bank[:], qv_w[:].bitcast(FP8X4), qv_s[:], fp4(keys_w, lo, hi), keys_s[:, lo:hi])
+            nc.scalar.activation(a[:, lo:hi], bank[:], COPY)
+        ag = sb.tile([P, SLOTS], F32, name="ag")
+        for h in range(2):
+            nc.scalar.activation(ag[:, h * HALF : (h + 1) * HALF], a[:].indirect(half(l1, h)), COPY)
+
+        dd = sb.tile([P, POOL], F32, name="dd")
+        for j in range(2):
+            lo, hi = j * BANK, (j + 1) * BANK
+            bank = ps.tile([P, BANK], F32, name="d_ps", tag="bank%d" % (4 + j))
+            score(bank[:], st_w[:].bitcast(FP8X4), st_s[:], fp8(shelves_w, lo, hi), shelves_s[:, lo:hi])
+            nc.vector.tensor_tensor(dd[:, lo:hi], bank[:], f2[:, lo:hi], ALU.subtract)
+        dg = sb.tile([P, SLOTS], F32, name="dg", tag="a")
+        nc.scalar.activation(dg[:], dd[:].indirect(l6[:]), COPY)
+
+        for h in range(2):
+            nc.vector.tensor_copy(f1[:].indirect(half(l2, h)), ag[:, h * HALF : (h + 1) * HALF])
+
+        bb = sb.tile([P, POOL], F32, name="bb")
+        for j in range(2):
+            lo, hi = j * BANK, (j + 1) * BANK
+            bank = ps.tile([P, BANK], F32, name="b_ps", tag="bank%d" % (6 + j))
+            score(bank[:], qv_w[:].bitcast(FP8X4), qv_s[:], fp8(notes_w, lo, hi), notes_s[:, lo:hi])
+            nc.vector.tensor_tensor(bb[:, lo:hi], bank[:], f1[:, lo:hi], ALU.add)
+
+        bg = sb.tile([P, SLOTS], F32, name="bg")
+        nc.vector.tensor_copy(bg[:, :HALF], bb[:].indirect(half(l5, 0)))
+        nc.scalar.activation(bg[:, HALF:], bb[:].indirect(half(l5, 1)), COPY)
+        y = sb.tile([P, SLOTS], F32, name="y")
+        for h in range(2):
+            cols = slice(h * HALF, (h + 1) * HALF)
+            nc.vector.tensor_tensor(y[:, cols], bg[:, cols], dg[:, cols], ALU.max)
+            nc.sync.dma_start(out[:, cols], y[:, cols])

@@ -1,7 +1,6 @@
 from contextlib import ExitStack
 
 import concourse.mybir as mybir
-from concourse.masks import make_identity
 
 F32 = mybir.dt.float32
 BF16 = mybir.dt.bfloat16
@@ -23,6 +22,8 @@ SLOTS = 512
 BANK = 512
 HALF = SLOTS // 2
 LCOLS = SLOTS // 16
+GP_COLS = 256
+EARLY = 192
 
 FLOPS = 2 * 512 * Q * (KQ + 4 * POOL)
 
@@ -52,10 +53,12 @@ def tile_attend_twomarkets_madefour_kernel(
             nc.sync.dma_start(t[:].bitcast(I32), src[0].bitcast(I32))
             return t
 
-        def load_plane(queue, src, width, name):
+        def load_plane(queues, src, width, name, clear=False):
             t = sb.tile([P, width], U8, name=name, align_bytes=64)
+            if clear:
+                nc.vector.memset(t[:].bitcast(U32), 0)
             for g in range(4):
-                queue.dma_start(t[32 * g : 32 * g + 4, :].bitcast(I32), src[0, 4 * g : 4 * g + 4, :].bitcast(I32))
+                queues[g].dma_start(t[32 * g : 32 * g + 4, :].bitcast(I32), src[0, 4 * g : 4 * g + 4, :].bitcast(I32))
             return t
 
         def half(lst, h):
@@ -63,36 +66,41 @@ def tile_attend_twomarkets_madefour_kernel(
 
         st_raw = sb.tile([P, PACK, Q], F32, name="st_raw")
         nc.sync.dma_start(st_raw[:], states.rearrange("(p j) q -> p j q", j=PACK))
-        users_s = load_plane(nc.scalar, users_scales, POOL, "users_s")
+        users_s = load_plane([nc.scalar] * 4, users_scales, POOL, "users_s")
         users_w = load_words4(users_words, "users_w")
         wq_w = load_words8(wq_words, KQ, "wq_w")
-        wq_s = load_plane(nc.sync, wq_scales, KQ, "wq_s")
+        wq_s = load_plane([nc.sync] * 4, wq_scales, KQ, "wq_s", clear=True)
         l3 = load_list(offs3, "l3")
         l4 = load_list(offs4, "l4")
         keys_w = load_words4(keys_words, "keys_w")
-        keys_s = load_plane(nc.sync, keys_scales, POOL, "keys_s")
+        keys_s = load_plane([nc.sync, nc.sync, nc.gpsimd, nc.gpsimd], keys_scales, POOL, "keys_s")
         shelves_w = load_words8(shelves_words, POOL, "shelves_w")
-        shelves_s = load_plane(nc.sync, shelves_scales, POOL, "shelves_s")
+        shelves_s = load_plane([nc.sync] * 4, shelves_scales, POOL, "shelves_s")
         l1 = load_list(offs, "l1")
         l2 = load_list(offs2, "l2")
         notes_w = load_words8(notes_words, POOL, "notes_w")
-        notes_s = load_plane(nc.sync, notes_scales, POOL, "notes_s")
+        notes_s = load_plane([nc.sync] * 4, notes_scales, POOL, "notes_s")
         l6 = load_list(offs6, "l6")
         l5 = load_list(offs5, "l5")
 
-        ident = sb.tile([P, P], F32, name="ident")
-        make_identity(nc, ident[:])
 
         f2 = sb.tile([P, POOL], F32, name="f2")
         f1 = sb.tile([P, POOL], F32, name="f1")
         nc.vector.memset(f2[:], 0.0)
         nc.vector.memset(f1[:], 0.0)
+        ones = sb.tile([P, EARLY], F32, name="ones")
+        nc.vector.memset(ones[:], 1.0)
 
         st_b = sb.tile([P, Q, PACK], BF16, name="st_b", align_bytes=64)
-        nc.vector.tensor_copy(st_b[:], st_raw[:].rearrange("p j q -> p q j"))
         st_w = sb.tile([P, Q], U32, name="st_w", align_bytes=64)
         st_s = sb.tile([P, Q], U8, name="st_s", align_bytes=64)
-        nc.vector.quantize_mx(st_w[:].bitcast(FP8X4), st_s[:], st_b[:].rearrange("p q j -> p (q j)"))
+        q_halves = [slice(0, Q // 2), slice(Q // 2, Q)]
+        for cols in q_halves:
+            nc.vector.tensor_copy(st_b[:, cols, :], st_raw[:, :, cols].rearrange("p j q -> p q j"))
+        for cols in q_halves:
+            nc.vector.quantize_mx(
+                st_w[:, cols].bitcast(FP8X4), st_s[:, cols], st_b[:, cols, :].rearrange("p q j -> p (q j)")
+            )
 
         def score(bank, lhs_w, lhs_s, rhs, rhs_s):
             nc.tensor.matmul_mx(bank, lhsT=lhs_w, lhsT_scale=lhs_s, rhs=rhs, rhs_scale=rhs_s, start=True, stop=True)
@@ -103,39 +111,43 @@ def tile_attend_twomarkets_madefour_kernel(
         def fp8(words, lo, hi):
             return words[:, lo:hi].bitcast(FP8X4)
 
+        wqd_w = sb.tile([P, KQ], U32, name="wqd_w", tag="wqd_w", align_bytes=64)
+        nc.scalar.copy(
+            wqd_w[:].rearrange("p (t m) -> p t m", t=PACK), wq_w[:].rearrange("p (m t) -> p t m", t=PACK)
+        )
+
         c0 = sb.tile([P, POOL], F32, name="c0")
         quarter = POOL // 4
         for j in range(4):
             lo, hi = j * quarter, (j + 1) * quarter
             bank = ps.tile([P, quarter], F32, name="c0_ps", tag="bank%d" % j)
             score(bank[:], st_w[:].bitcast(FP8X4), st_s[:], fp4(users_w, lo, hi), users_s[:, lo:hi])
-            if j % 2 == 0:
+            if j >= 2:
                 nc.scalar.activation(c0[:, lo:hi], bank[:], COPY)
             else:
                 nc.vector.tensor_copy(c0[:, lo:hi], bank[:])
 
-        qt_ps = ps.tile([P, KQ], F32, name="qt_ps", tag="bank4")
-        score(qt_ps[:], st_w[:].bitcast(FP8X4), st_s[:], fp8(wq_w, 0, KQ), wq_s[:])
+        wqd_s = sb.tile([P, KQ], U8, name="wqd_s", align_bytes=64)
+        nc.vector.tensor_copy(
+            wqd_s[:].rearrange("p (t m) -> p t m", t=PACK), wq_s[:].rearrange("p (m t) -> p t m", t=PACK)
+        )
+        qv_ps = ps.tile([P, PACK, Q], F32, name="qv_ps", tag="bank4")
+        for t in range(PACK):
+            score(qv_ps[:, t, :], fp8(wqd_w, t * P, (t + 1) * P), wqd_s[:, t * P : (t + 1) * P], st_w[:].bitcast(FP8X4), st_s[:])
 
-        cg0 = sb.tile([P, HALF], F32, name="cg0")
-        nc.vector.tensor_copy(cg0[:], c0[:].indirect(half(l3, 0)))
-        nc.vector.tensor_copy(f2[:].indirect(half(l4, 0)), cg0[:])
+        cg0 = sb.tile([P, EARLY], F32, name="cg0")
+        nc.vector.tensor_tensor(cg0[:], c0[:].indirect(l3[:, : EARLY // 16]), ones[:], ALU.mult)
 
-        qt_b = sb.tile([P, 2, P, 2], BF16, name="qt_b", tag="qt_b")
-        nc.scalar.activation(qt_b[:], qt_ps[:].rearrange("q (p u e) -> q u p e", u=2, e=2), COPY)
-        qt_words = qt_b[:].rearrange("q u p e -> q (u p e)").bitcast(F32)
-        qv_ps = ps.tile([P, 2, Q], F32, name="qv_ps", tag="bank5")
-        for u in range(2):
-            nc.tensor.transpose(qv_ps[:, u, :], qt_words[:, u * P : (u + 1) * P], ident[:])
-        qv_b = sb.tile([P, Q * PACK], BF16, name="qv_b", align_bytes=64)
-        nc.scalar.copy(qv_b[:].bitcast(F32).rearrange("p (q u) -> p q u", u=2), qv_ps[:].rearrange("p u q -> p q u"))
+        qv_b = sb.tile([P, Q, PACK], BF16, name="qv_b", align_bytes=64)
+        nc.scalar.activation(qv_b[:], qv_ps[:].rearrange("p t q -> p q t"), COPY)
+        nc.vector.tensor_copy(f2[:].indirect(l4[:, : EARLY // 16]), cg0[:])
         qv_w = sb.tile([P, Q], U32, name="qv_w", align_bytes=64)
         qv_s = sb.tile([P, Q], U8, name="qv_s", align_bytes=64)
-        nc.vector.quantize_mx(qv_w[:].bitcast(FP8X4), qv_s[:], qv_b[:])
+        nc.vector.quantize_mx(qv_w[:].bitcast(FP8X4), qv_s[:], qv_b[:].rearrange("p q j -> p (q j)"))
 
-        cg1 = sb.tile([P, HALF], F32, name="cg1", tag="qt_b")
-        nc.scalar.activation(cg1[:], c0[:].indirect(half(l3, 1)), COPY)
-        nc.vector.tensor_copy(f2[:].indirect(half(l4, 1)), cg1[:])
+        cg1 = sb.tile([P, SLOTS - EARLY], F32, name="cg1", tag="wqd_w", align_bytes=64)
+        nc.scalar.activation(cg1[:], c0[:].indirect(l3[:, EARLY // 16 :]), COPY)
+        nc.vector.tensor_copy(f2[:].indirect(l4[:, EARLY // 16 :]), cg1[:])
         a = sb.tile([P, POOL], F32, name="a", tag="a")
         for j in range(4):
             lo, hi = j * quarter, (j + 1) * quarter
@@ -143,27 +155,38 @@ def tile_attend_twomarkets_madefour_kernel(
             score(bank[:], qv_w[:].bitcast(FP8X4), qv_s[:], fp4(keys_w, lo, hi), keys_s[:, lo:hi])
             nc.scalar.activation(a[:, lo:hi], bank[:], COPY)
         ag = sb.tile([P, SLOTS], F32, name="ag")
-        for h in range(2):
-            nc.scalar.activation(ag[:, h * HALF : (h + 1) * HALF], a[:].indirect(half(l1, h)), COPY)
+        nc.scalar.activation(ag[:, :HALF], a[:].indirect(half(l1, 0)), COPY)
 
         dd = sb.tile([P, POOL], F32, name="dd")
-        for j in range(2):
-            lo, hi = j * BANK, (j + 1) * BANK
-            bank = ps.tile([P, BANK], F32, name="d_ps", tag="bank%d" % (4 + j))
+        late = BANK
+        for j, (lo, hi) in enumerate(((0, BANK),)):
+            bank = ps.tile([P, hi - lo], F32, name="d_ps", tag="bank%d" % j)
             score(bank[:], st_w[:].bitcast(FP8X4), st_s[:], fp8(shelves_w, lo, hi), shelves_s[:, lo:hi])
             nc.vector.tensor_tensor(dd[:, lo:hi], bank[:], f2[:, lo:hi], ALU.subtract)
+        nc.vector.tensor_copy(f1[:].indirect(half(l2, 0)), ag[:, :HALF])
+        bank = ps.tile([P, POOL - late], F32, name="d_ps", tag="bank3")
+        score(bank[:], st_w[:].bitcast(FP8X4), st_s[:], fp8(shelves_w, late, POOL), shelves_s[:, late:])
+        d_late = sb.tile([P, POOL - late], F32, name="d_late")
+        nc.scalar.activation(d_late[:], bank[:], COPY)
+        nc.vector.tensor_tensor(dd[:, late:], d_late[:], f2[:, late:], ALU.subtract)
+        nc.scalar.activation(ag[:, HALF:], a[:].indirect(half(l1, 1)), COPY)
+        nc.vector.tensor_copy(f1[:].indirect(half(l2, 1)), ag[:, HALF:])
         dg = sb.tile([P, SLOTS], F32, name="dg", tag="a")
         nc.scalar.activation(dg[:], dd[:].indirect(l6[:]), COPY)
 
-        for h in range(2):
-            nc.vector.tensor_copy(f1[:].indirect(half(l2, h)), ag[:, h * HALF : (h + 1) * HALF])
-
         bb = sb.tile([P, POOL], F32, name="bb")
+        b_ps = []
         for j in range(2):
             lo, hi = j * BANK, (j + 1) * BANK
-            bank = ps.tile([P, BANK], F32, name="b_ps", tag="bank%d" % (6 + j))
+            bank = ps.tile([P, BANK], F32, name="b_ps", tag="bank%d" % (1 - j))
             score(bank[:], qv_w[:].bitcast(FP8X4), qv_s[:], fp8(notes_w, lo, hi), notes_s[:, lo:hi])
-            nc.vector.tensor_tensor(bb[:, lo:hi], bank[:], f1[:, lo:hi], ALU.add)
+            b_ps.append(bank)
+        cut = POOL - GP_COLS
+        b_tail = sb.tile([P, GP_COLS], F32, name="b_tail")
+        nc.scalar.activation(b_tail[:], b_ps[1][:, cut - BANK :], COPY)
+        nc.vector.tensor_tensor(bb[:, :BANK], b_ps[0][:], f1[:, :BANK], ALU.add)
+        nc.vector.tensor_tensor(bb[:, BANK:cut], b_ps[1][:, : cut - BANK], f1[:, BANK:cut], ALU.add)
+        nc.gpsimd.tensor_tensor(bb[:, cut:], b_tail[:], f1[:, cut:], ALU.add)
 
         bg = sb.tile([P, SLOTS], F32, name="bg")
         nc.vector.tensor_copy(bg[:, :HALF], bb[:].indirect(half(l5, 0)))

@@ -113,7 +113,8 @@ def tile_attend_twomarkets_madefour_kernel(
 
         wqd_w = sb.tile([P, KQ], U32, name="wqd_w", tag="wqd_w", align_bytes=64)
         nc.scalar.copy(
-            wqd_w[:].rearrange("p (t m) -> p t m", t=PACK), wq_w[:].rearrange("p (m t) -> p t m", t=PACK)
+            wqd_w[:].rearrange("p (t b i) -> p b t i", t=PACK, i=4),
+            wq_w[:].rearrange("p (b i t) -> p b t i", t=PACK, i=4),
         )
 
         c0 = sb.tile([P, POOL], F32, name="c0")
@@ -168,7 +169,7 @@ def tile_attend_twomarkets_madefour_kernel(
         score(bank[:], st_w[:].bitcast(FP8X4), st_s[:], fp8(shelves_w, late, POOL), shelves_s[:, late:])
         d_late = sb.tile([P, POOL - late], F32, name="d_late")
         nc.scalar.activation(d_late[:], bank[:], COPY)
-        nc.vector.tensor_tensor(dd[:, late:], d_late[:], f2[:, late:], ALU.subtract)
+        nc.gpsimd.tensor_tensor(dd[:, late:], d_late[:], f2[:, late:], ALU.subtract)
         nc.scalar.activation(ag[:, HALF:], a[:].indirect(half(l1, 1)), COPY)
         nc.vector.tensor_copy(f1[:].indirect(half(l2, 1)), ag[:, HALF:])
         dg = sb.tile([P, SLOTS], F32, name="dg", tag="a")

from contextlib import ExitStack

import concourse.mybir as mybir

F32 = mybir.dt.float32
BF16 = mybir.dt.bfloat16
I32 = mybir.dt.int32
U32 = mybir.dt.uint32
U16 = mybir.dt.uint16
U8 = mybir.dt.uint8
FP8X4 = mybir.dt.float8_e4m3fn_x4
FP4X4 = mybir.dt.float4_e2m1fn_x4
COPY = mybir.ActivationFunctionType.Copy
ALU = mybir.AluOpType

P = 128
PACK = 4
Q = 128
KQ = 512
POOL = 1024
SLOTS = 512
BANK = 512
HALF = SLOTS // 2
LCOLS = SLOTS // 16
GP_COLS = 256
EARLY = 192

FLOPS = 2 * 512 * Q * (KQ + 4 * POOL)


def tile_attend_twomarkets_madefour_kernel(
    tc, states, wq_words, wq_scales, keys_words, keys_scales, notes_words, notes_scales,
    users_words, users_scales, shelves_words, shelves_scales,
    offs, offs2, offs3, offs4, offs5, offs6, out,
):
    nc = tc.nc
    with ExitStack() as ctx:
        sb = ctx.enter_context(tc.tile_pool(name="sb", bufs=1))
        ps = ctx.enter_context(tc.psum_pool(name="ps", bufs=1))

        def load_list(src, name):
            t = sb.tile([P, LCOLS], U16, name=name)
            nc.sync.dma_start(t[:], src)
            return t

        def load_words8(src, width, name):
            t = sb.tile([P, width], U32, name=name, align_bytes=64)
            nc.sync.dma_start(t[:].bitcast(I32), src[0].rearrange("p n t -> p (n t)").bitcast(I32))
            return t

        def load_words4(src, name):
            t = sb.tile([P, 2 * POOL], U8, name=name, align_bytes=64)
            nc.sync.dma_start(t[:].bitcast(I32), src[0].bitcast(I32))
            return t

        def load_plane(queues, src, width, name, clear=False):
            t = sb.tile([P, width], U8, name=name, align_bytes=64)
            if clear:
                nc.vector.memset(t[:].bitcast(U32), 0)
            for g in range(4):
                queues[g].dma_start(t[32 * g : 32 * g + 4, :].bitcast(I32), src[0, 4 * g : 4 * g + 4, :].bitcast(I32))
            return t

        def half(lst, h):
            return lst[:, h * (LCOLS // 2) : (h + 1) * (LCOLS // 2)]

        st_raw = sb.tile([P, PACK, Q], F32, name="st_raw")
        nc.sync.dma_start(st_raw[:], states.rearrange("(p j) q -> p j q", j=PACK))
        users_s = load_plane([nc.scalar] * 4, users_scales, POOL, "users_s")
        users_w = load_words4(users_words, "users_w")
        wq_w = load_words8(wq_words, KQ, "wq_w")
        wq_s = load_plane([nc.sync] * 4, wq_scales, KQ, "wq_s", clear=True)
        l3 = load_list(offs3, "l3")
        l4 = load_list(offs4, "l4")
        keys_w = load_words4(keys_words, "keys_w")
        keys_s = load_plane([nc.sync, nc.sync, nc.gpsimd, nc.gpsimd], keys_scales, POOL, "keys_s")
        shelves_w = load_words8(shelves_words, POOL, "shelves_w")
        shelves_s = load_plane([nc.sync] * 4, shelves_scales, POOL, "shelves_s")
        l1 = load_list(offs, "l1")
        l2 = load_list(offs2, "l2")
        notes_w = load_words8(notes_words, POOL, "notes_w")
        notes_s = load_plane([nc.sync] * 4, notes_scales, POOL, "notes_s")
        l6 = load_list(offs6, "l6")
        l5 = load_list(offs5, "l5")


        f2 = sb.tile([P, POOL], F32, name="f2")
        f1 = sb.tile([P, POOL], F32, name="f1")
        nc.vector.memset(f2[:], 0.0)
        nc.vector.memset(f1[:], 0.0)
        ones = sb.tile([P, EARLY], F32, name="ones")
        nc.vector.memset(ones[:], 1.0)

        st_b = sb.tile([P, Q, PACK], BF16, name="st_b", align_bytes=64)
        st_w = sb.tile([P, Q], U32, name="st_w", align_bytes=64)
        st_s = sb.tile([P, Q], U8, name="st_s", align_bytes=64)
        q_halves = [slice(0, Q // 2), slice(Q // 2, Q)]
        for cols in q_halves:
            nc.vector.tensor_copy(st_b[:, cols, :], st_raw[:, :, cols].rearrange("p j q -> p q j"))
        for cols in q_halves:
            nc.vector.quantize_mx(
                st_w[:, cols].bitcast(FP8X4), st_s[:, cols], st_b[:, cols, :].rearrange("p q j -> p (q j)")
            )

        def score(bank, lhs_w, lhs_s, rhs, rhs_s):
            nc.tensor.matmul_mx(bank, lhsT=lhs_w, lhsT_scale=lhs_s, rhs=rhs, rhs_scale=rhs_s, start=True, stop=True)

        def fp4(words, lo, hi):
            return words[:, 2 * lo : 2 * hi].bitcast(FP4X4)

        def fp8(words, lo, hi):
            return words[:, lo:hi].bitcast(FP8X4)

        wqd_w = sb.tile([P, KQ], U32, name="wqd_w", tag="wqd_w", align_bytes=64)
        nc.scalar.copy(
            wqd_w[:].rearrange("p (t b i) -> p b t i", t=PACK, i=4),
            wq_w[:].rearrange("p (b i t) -> p b t i", t=PACK, i=4),
        )

        c0 = sb.tile([P, POOL], F32, name="c0")
        quarter = POOL // 4
        for j in range(4):
            lo, hi = j * quarter, (j + 1) * quarter
            bank = ps.tile([P, quarter], F32, name="c0_ps", tag="bank%d" % j)
            score(bank[:], st_w[:].bitcast(FP8X4), st_s[:], fp4(users_w, lo, hi), users_s[:, lo:hi])
            if j >= 2:
                nc.scalar.activation(c0[:, lo:hi], bank[:], COPY)
            else:
                nc.vector.tensor_copy(c0[:, lo:hi], bank[:])

        wqd_s = sb.tile([P, KQ], U8, name="wqd_s", align_bytes=64)
        nc.vector.tensor_copy(
            wqd_s[:].rearrange("p (t m) -> p t m", t=PACK), wq_s[:].rearrange("p (m t) -> p t m", t=PACK)
        )
        qv_ps = ps.tile([P, PACK, Q], F32, name="qv_ps", tag="bank4")
        for t in range(PACK):
            score(qv_ps[:, t, :], fp8(wqd_w, t * P, (t + 1) * P), wqd_s[:, t * P : (t + 1) * P], st_w[:].bitcast(FP8X4), st_s[:])

        cg0 = sb.tile([P, EARLY], F32, name="cg0")
        nc.vector.tensor_tensor(cg0[:], c0[:].indirect(l3[:, : EARLY // 16]), ones[:], ALU.mult)

        qv_b = sb.tile([P, Q, PACK], BF16, name="qv_b", align_bytes=64)
        nc.scalar.activation(qv_b[:], qv_ps[:].rearrange("p t q -> p q t"), COPY)
        nc.vector.tensor_copy(f2[:].indirect(l4[:, : EARLY // 16]), cg0[:])
        qv_w = sb.tile([P, Q], U32, name="qv_w", align_bytes=64)
        qv_s = sb.tile([P, Q], U8, name="qv_s", align_bytes=64)
        nc.vector.quantize_mx(qv_w[:].bitcast(FP8X4), qv_s[:], qv_b[:].rearrange("p q j -> p (q j)"))

        cg1 = sb.tile([P, SLOTS - EARLY], F32, name="cg1", tag="wqd_w", align_bytes=64)
        nc.scalar.activation(cg1[:], c0[:].indirect(l3[:, EARLY // 16 :]), COPY)
        nc.vector.tensor_copy(f2[:].indirect(l4[:, EARLY // 16 :]), cg1[:])
        a = sb.tile([P, POOL], F32, name="a", tag="a")
        for j in range(4):
            lo, hi = j * quarter, (j + 1) * quarter
            bank = ps.tile([P, quarter], F32, name="a_ps", tag="bank%d" % j)
            score(bank[:], qv_w[:].bitcast(FP8X4), qv_s[:], fp4(keys_w, lo, hi), keys_s[:, lo:hi])
            nc.scalar.activation(a[:, lo:hi], bank[:], COPY)
        ag = sb.tile([P, SLOTS], F32, name="ag")
        nc.scalar.activation(ag[:, :HALF], a[:].indirect(half(l1, 0)), COPY)

        dd = sb.tile([P, POOL], F32, name="dd")
        late = BANK
        for j, (lo, hi) in enumerate(((0, BANK),)):
            bank = ps.tile([P, hi - lo], F32, name="d_ps", tag="bank%d" % j)
            score(bank[:], st_w[:].bitcast(FP8X4), st_s[:], fp8(shelves_w, lo, hi), shelves_s[:, lo:hi])
            nc.vector.tensor_tensor(dd[:, lo:hi], bank[:], f2[:, lo:hi], ALU.subtract)
        nc.vector.tensor_copy(f1[:].indirect(half(l2, 0)), ag[:, :HALF])
        bank = ps.tile([P, POOL - late], F32, name="d_ps", tag="bank3")
        score(bank[:], st_w[:].bitcast(FP8X4), st_s[:], fp8(shelves_w, late, POOL), shelves_s[:, late:])
        d_late = sb.tile([P, POOL - late], F32, name="d_late")
        nc.scalar.activation(d_late[:], bank[:], COPY)
        nc.gpsimd.tensor_tensor(dd[:, late:], d_late[:], f2[:, late:], ALU.subtract)
        nc.scalar.activation(ag[:, HALF:], a[:].indirect(half(l1, 1)), COPY)
        nc.vector.tensor_copy(f1[:].indirect(half(l2, 1)), ag[:, HALF:])
        dg = sb.tile([P, SLOTS], F32, name="dg", tag="a")
        nc.scalar.activation(dg[:], dd[:].indirect(l6[:]), COPY)

        bb = sb.tile([P, POOL], F32, name="bb")
        b_ps = []
        for j in range(2):
            lo, hi = j * BANK, (j + 1) * BANK
            bank = ps.tile([P, BANK], F32, name="b_ps", tag="bank%d" % (1 - j))
            score(bank[:], qv_w[:].bitcast(FP8X4), qv_s[:], fp8(notes_w, lo, hi), notes_s[:, lo:hi])
            b_ps.append(bank)
        cut = POOL - GP_COLS
        b_tail = sb.tile([P, GP_COLS], F32, name="b_tail")
        nc.scalar.activation(b_tail[:], b_ps[1][:, cut - BANK :], COPY)
        nc.vector.tensor_tensor(bb[:, :BANK], b_ps[0][:], f1[:, :BANK], ALU.add)
        nc.vector.tensor_tensor(bb[:, BANK:cut], b_ps[1][:, : cut - BANK], f1[:, BANK:cut], ALU.add)
        nc.gpsimd.tensor_tensor(bb[:, cut:], b_tail[:], f1[:, cut:], ALU.add)

        bg = sb.tile([P, SLOTS], F32, name="bg")
        nc.vector.tensor_copy(bg[:, :HALF], bb[:].indirect(half(l5, 0)))
        nc.scalar.activation(bg[:, HALF:], bb[:].indirect(half(l5, 1)), COPY)
        y = sb.tile([P, SLOTS], F32, name="y")
        for h in range(2):
            cols = slice(h * HALF, (h + 1) * HALF)
            nc.vector.tensor_tensor(y[:, cols], bg[:, cols], dg[:, cols], ALU.max)
            nc.sync.dma_start(out[:, cols], y[:, cols])
